import numpy as np
CORES = [4,5,6,7,12,13,14,15,20,21,22,23,28,29,30,31]
N = 16
ROOT = 14
def setup_inputs(rng):
    return {"x": rng.standard_normal((N, 128, 128), dtype=np.float32)}
def reference(x):
    y = np.full(x.shape, np.nan, x.dtype)
    y[ROOT] = x.min(axis=0)
    return {"y": y}

@@ -1,0 +1,52 @@
+from concourse.bass import DstId, RemoteDMATransfer
+
+SCRATCH = {
+    "own": ("dram", [128, 128], "float32"),
+    "land": ("dram", [6, 128, 128], "float32"),
+    "res": ("dram", [128, 128], "float32"),
+}
+SEMAPHORES = ["loaded", "sent", "arrived", "stored"]
+
+MIN = 3
+ROOT_CORE = 30
+LAST = 31
+
+
+def rank_program(g, core, T, topo):
+    rank = T.rank_of(core)
+    if rank is None:
+        return
+    ch = topo.chip(core)
+    gather = ch * 8 + 7
+
+    g.sync.dma_start(T.own[:], T.x[:]).then_inc(T.sem.loaded, 16)
+    g.wait_ge(T.sem.loaded, 16)
+
+    if core != gather:
+        rid, pid, _ = topo.addr(gather)
+        g.remote_dma(T.land[core % 8 - 4], T.own[:], T.sem.arrived, T.sem.sent, pid, rid, 0xFFFF)
+        g.wait_ge(T.sem.sent, 16)
+        if core == ROOT_CORE:
+            g.wait_ge(T.sem.arrived, 16)
+            g.sync.wait_ge(T.sem.arrived, 16)
+            g.sync.dma_start(T.y[:], T.res[:]).then_inc(T.sem.stored, 16)
+            g.wait_ge(T.sem.stored, 16)
+        return
+
+    if core != LAST:
+        g.wait_ge(T.sem.arrived, 3 * 16)
+        rid, pid, _ = topo.addr(LAST)
+        g.remote_dma_fused(
+            [RemoteDMATransfer(dst_ids=[DstId(rid=rid, pnc=pid)], dma_engine_mask=0x00FF, remote_sem=T.sem.arrived,
+                               srcs=[T.own[:], T.land[0], T.land[1], T.land[2]], dsts=[T.land[3 + ch]], alu_op=MIN)],
+            local_sem=T.sem.sent)
+        g.wait_ge(T.sem.sent, 8)
+        return
+
+    g.wait_ge(T.sem.arrived, 3 * 16 + 3 * 8)
+    rid, pid, _ = topo.addr(ROOT_CORE)
+    g.remote_dma_fused(
+        [RemoteDMATransfer(dst_ids=[DstId(rid=rid, pnc=pid)], dma_engine_mask=0xFFFF, remote_sem=T.sem.arrived,
+                           srcs=[T.own[:]] + [T.land[k] for k in range(6)], dsts=[T.res[:]], alu_op=MIN)],
+        local_sem=T.sem.sent)
+    g.wait_ge(T.sem.sent, 16)

@@ -1,52 +1,78 @@
 from concourse.bass import DstId, RemoteDMATransfer
 
+PIECES = 4
+ROOT_CORE = 30
+MIN = 3
+GATHER = (
+    (6, 12, 22, 28),
+    (2, 8, 18, 29),
+    (7, 14, 23, 31),
+    (3, 10, 19, 27),
+)
+FINAL_CHIP = (3, 3, 2, 2)
+
 SCRATCH = {
-    "own": ("dram", [128, 128], "float32"),
-    "land": ("dram", [6, 128, 128], "float32"),
-    "res": ("dram", [128, 128], "float32"),
+    "own": ("dram", [PIECES, 128, 32], "float32"),
+    "land": ("dram", [8, 128, 32], "float32"),
+    "res": ("dram", [PIECES, 128, 32], "float32"),
 }
 SEMAPHORES = ["loaded", "sent", "arrived", "stored"]
 
-MIN = 3
-ROOT_CORE = 30
-LAST = 31
-
 
 def rank_program(g, core, T, topo):
-    rank = T.rank_of(core)
-    if rank is None:
-        return
-    ch = topo.chip(core)
-    gather = ch * 8 + 7
-
-    g.sync.dma_start(T.own[:], T.x[:]).then_inc(T.sem.loaded, 16)
-    g.wait_ge(T.sem.loaded, 16)
-
-    if core != gather:
-        rid, pid, _ = topo.addr(gather)
-        g.remote_dma(T.land[core % 8 - 4], T.own[:], T.sem.arrived, T.sem.sent, pid, rid, 0xFFFF)
-        g.wait_ge(T.sem.sent, 16)
-        if core == ROOT_CORE:
-            g.wait_ge(T.sem.arrived, 16)
-            g.sync.wait_ge(T.sem.arrived, 16)
-            g.sync.dma_start(T.y[:], T.res[:]).then_inc(T.sem.stored, 16)
-            g.wait_ge(T.sem.stored, 16)
+    chip = topo.chip(core)
+    is_rank = T.rank_of(core) is not None
+    my_piece = [p for p in range(PIECES) if GATHER[p][chip] == core]
+    if not is_rank and not my_piece:
         return
 
-    if core != LAST:
-        g.wait_ge(T.sem.arrived, 3 * 16)
-        rid, pid, _ = topo.addr(LAST)
+    def dst(c):
+        rid, pid, _ = topo.addr(c)
+        return DstId(rid=rid, pnc=pid)
+
+    sent = 0
+
+    if is_rank:
+        g.sync.dma_start(T.own[:], T.x[:]).then_inc(T.sem.loaded, 16)
+        g.wait_ge(T.sem.loaded, 16)
+        transfers = []
+        for p in range(PIECES):
+            if GATHER[p][chip] != core:
+                transfers.append(RemoteDMATransfer(
+                    dst_ids=[dst(GATHER[p][chip])], dma_engine_mask=0xF << (4 * p), remote_sem=T.sem.arrived,
+                    src=T.own[p], dst=T.land[core % 8 - 4], alu_op=0))
+        g.remote_dma_fused(transfers, local_sem=T.sem.sent)
+        sent += 4 * len(transfers)
+
+    if my_piece:
+        p = my_piece[0]
+        srcs, expect = [], 0
+        for c in range(chip * 8 + 4, chip * 8 + 8):
+            if c == core:
+                srcs.append(T.own[p])
+            else:
+                srcs.append(T.land[c % 8 - 4])
+                expect += 4
+        if chip == FINAL_CHIP[p]:
+            for ch in range(4):
+                if ch != chip:
+                    srcs.append(T.land[4 + ch])
+                    expect += 8
+            target, out = ROOT_CORE, T.res[p]
+        else:
+            target, out = GATHER[p][FINAL_CHIP[p]], T.land[4 + chip]
+        mask = topo.mask(core, target)
+        g.wait_ge(T.sem.arrived, expect)
         g.remote_dma_fused(
-            [RemoteDMATransfer(dst_ids=[DstId(rid=rid, pnc=pid)], dma_engine_mask=0x00FF, remote_sem=T.sem.arrived,
-                               srcs=[T.own[:], T.land[0], T.land[1], T.land[2]], dsts=[T.land[3 + ch]], alu_op=MIN)],
+            [RemoteDMATransfer(dst_ids=[dst(target)], dma_engine_mask=mask, remote_sem=T.sem.arrived,
+                               srcs=srcs, dsts=[out], alu_op=MIN)],
             local_sem=T.sem.sent)
-        g.wait_ge(T.sem.sent, 8)
-        return
+        sent += 16 if mask == 0xFFFF else 8
 
-    g.wait_ge(T.sem.arrived, 3 * 16 + 3 * 8)
-    rid, pid, _ = topo.addr(ROOT_CORE)
-    g.remote_dma_fused(
-        [RemoteDMATransfer(dst_ids=[DstId(rid=rid, pnc=pid)], dma_engine_mask=0xFFFF, remote_sem=T.sem.arrived,
-                           srcs=[T.own[:]] + [T.land[k] for k in range(6)], dsts=[T.res[:]], alu_op=MIN)],
-        local_sem=T.sem.sent)
-    g.wait_ge(T.sem.sent, 16)
+    if core == ROOT_CORE:
+        expect = sum(16 if FINAL_CHIP[p] == chip else 8 for p in range(PIECES))
+        g.sync.wait_ge(T.sem.arrived, expect)
+        g.sync.dma_start(T.y[:], T.res[:]).then_inc(T.sem.stored, 16)
+        g.wait_ge(T.sem.stored, 16)
+
+    g.wait_ge(T.sem.sent, sent)

from concourse.bass import DstId, RemoteDMATransfer

PIECES = 4
ROOT_CORE = 30
MIN = 3
GATHER = (
    (6, 12, 22, 28),
    (2, 8, 18, 29),
    (7, 14, 23, 31),
    (3, 10, 19, 27),
)
FINAL_CHIP = (3, 3, 2, 2)

SCRATCH = {
    "own": ("dram", [PIECES, 128, 32], "float32"),
    "land": ("dram", [8, 128, 32], "float32"),
    "res": ("dram", [PIECES, 128, 32], "float32"),
}
SEMAPHORES = ["loaded", "sent", "arrived", "stored"]


def rank_program(g, core, T, topo):
    chip = topo.chip(core)
    is_rank = T.rank_of(core) is not None
    my_piece = [p for p in range(PIECES) if GATHER[p][chip] == core]
    if not is_rank and not my_piece:
        return

    def dst(c):
        rid, pid, _ = topo.addr(c)
        return DstId(rid=rid, pnc=pid)

    sent = 0

    if is_rank:
        g.sync.dma_start(T.own[:], T.x[:]).then_inc(T.sem.loaded, 16)
        g.wait_ge(T.sem.loaded, 16)
        transfers = []
        for p in range(PIECES):
            if GATHER[p][chip] != core:
                transfers.append(RemoteDMATransfer(
                    dst_ids=[dst(GATHER[p][chip])], dma_engine_mask=0xF << (4 * p), remote_sem=T.sem.arrived,
                    src=T.own[p], dst=T.land[core % 8 - 4], alu_op=0))
        g.remote_dma_fused(transfers, local_sem=T.sem.sent)
        sent += 4 * len(transfers)

    if my_piece:
        p = my_piece[0]
        srcs, expect = [], 0
        for c in range(chip * 8 + 4, chip * 8 + 8):
            if c == core:
                srcs.append(T.own[p])
            else:
                srcs.append(T.land[c % 8 - 4])
                expect += 4
        if chip == FINAL_CHIP[p]:
            for ch in range(4):
                if ch != chip:
                    srcs.append(T.land[4 + ch])
                    expect += 8
            target, out = ROOT_CORE, T.res[p]
        else:
            target, out = GATHER[p][FINAL_CHIP[p]], T.land[4 + chip]
        mask = topo.mask(core, target)
        g.wait_ge(T.sem.arrived, expect)
        g.remote_dma_fused(
            [RemoteDMATransfer(dst_ids=[dst(target)], dma_engine_mask=mask, remote_sem=T.sem.arrived,
                               srcs=srcs, dsts=[out], alu_op=MIN)],
            local_sem=T.sem.sent)
        sent += 16 if mask == 0xFFFF else 8

    if core == ROOT_CORE:
        expect = sum(16 if FINAL_CHIP[p] == chip else 8 for p in range(PIECES))
        g.sync.wait_ge(T.sem.arrived, expect)
        g.sync.dma_start(T.y[:], T.res[:]).then_inc(T.sem.stored, 16)
        g.wait_ge(T.sem.stored, 16)

    g.wait_ge(T.sem.sent, sent)
